import numpy as np
CORES = [88,96,104,112,120,216,224,232,240,248]
N = 10
TK = 256
NT = N * TK
EPS = 0.01
def setup_inputs(rng):
    x = (rng.standard_normal((N, 128, TK), dtype=np.float32) * (0.5 + np.arange(N, dtype=np.float32).reshape(N, 1, 1) / N) + rng.standard_normal((N, 128, 1), dtype=np.float32))
    return {"x": x}
def setup_inputs_big(rng):
    d = setup_inputs(rng)
    for k in ("x",): d[k] = (d[k].astype(np.float32) * 1024.0).astype(d[k].dtype)
    return d
def setup_inputs_small(rng):
    d = setup_inputs(rng)
    for k in ("x",): d[k] = (d[k].astype(np.float32) * (1 / 1024.0)).astype(d[k].dtype)
    return d
def setup_inputs_apart(rng):
    d = setup_inputs(rng)
    f = (10.0 ** rng.permutation(np.linspace(-1.5, 1.5, N))).astype(np.float32).reshape(N, 1, 1)
    for k in ("x",): d[k] = (d[k].astype(np.float32) * f).astype(d[k].dtype)
    return d
def setup_inputs_mixed(rng):
    d = setup_inputs(rng)
    f = (10.0 ** rng.uniform(-3, 3, (1, 128, 1))).astype(np.float32); shape = rng.integers(3, size=(1, 128, 1))
    for k in ("x",):
        x = d[k].astype(np.float32)
        m = x.mean(axis=(0, 2), keepdims=True); level = m + np.sign(x - m) * np.abs(x - m).mean(axis=(0, 2), keepdims=True) * rng.uniform(0.9, 1.1, x.shape).astype(np.float32)
        other = x * np.where(rng.random(x.shape) < 0.5, 0.1, 1.0).astype(np.float32)
        d[k] = (np.where(shape == 1, level, np.where(shape == 2, other, x)) * f).astype(d[k].dtype)
    return d
def setup_inputs_offset(rng):
    d = setup_inputs(rng)
    x = d["x"]; spread = x.std(axis=(0, 2), keepdims=True)
    d["x"] = (x + spread * rng.uniform(16, 48, (1, 128, 1)) * rng.choice([-1.0, 1.0], (1, 128, 1))).astype(np.float32)
    return d
def reference(x):
    X = x.astype(np.float64)
    mu = X.sum(axis=(0, 2)).reshape(1, 128, 1) / NT
    rs = 1.0 / np.sqrt(((X - mu) ** 2).sum(axis=(0, 2)).reshape(1, 128, 1) / NT + EPS)
    n = (X - mu) * rs
    return {"y": n.astype(np.float32)}

@@ -1,0 +1,142 @@
+import math
+from concourse.bass import DstId, RemoteDMATransfer
+from concourse.mybir import AluOpType, ActivationFunctionType
+
+N = 10
+EPS = 0.01
+K1 = 8
+K2 = 4
+ROW_M2 = 32
+ROW_ONE = 64
+KK = ROW_ONE + 1
+
+SCRATCH = {
+    "xs": ("sbuf", [128, 256], "float32"),
+    "xm": ("sbuf", [128, 256], "float32"),
+    "ys": ("sbuf", [128, 256], "float32"),
+    "junk": ("sbuf", [128, 256], "float32"),
+    "j10": ("sbuf", [128, 16], "float32"),
+    "st": ("sbuf", [128, 2], "float32"),
+    "sc": ("sbuf", [128, 4], "float32"),
+    "tab": ("sbuf", [128, 260], "float32"),
+    "w": ("sbuf", [128, 12], "float32"),
+    "relay": ("dram", [128, 2], "float32"),
+    "gath": ("dram", [N, 128, 2], "float32"),
+    "ps": ("psum", [128, 512], "float32"),
+    "ps2": ("psum", [128, 512], "float32"),
+}
+SEMAPHORES = ["ld", "cst", "diag", "a", "harr", "sent", "hsent", "arr", "gl", "mm", "mm2", "p", "r", "xmd", "y1", "y2",
+              "stq"]
+
+
+def _bits(mask):
+    return [b for b in range(mask.bit_length()) if (mask >> b) & 1]
+
+
+def _relay_of(rank_core, cores, topo):
+    hosts = max(topo.host(c) for c in cores) + 1
+    cand = [c for c in range(hosts * topo.CORES_PER_HOST)
+            if c not in cores and topo.host(c) == topo.host(rank_core) and topo.chip(c) == topo.chip(rank_core)
+            and all(topo.may_write(c, d) for d in cores)]
+    near = [c for c in cand if topo.die(c) == topo.die(rank_core)]
+    return (near or cand)[0]
+
+
+def _relay_program(g, core, T, topo, r):
+    dests = list(T.cores)
+    common = topo.mask(core, dests[0])
+    for d in dests:
+        common &= topo.mask(core, d)
+    eng = _bits(common)
+    eng = eng[::len(eng) // K2][:K2]
+    transfers = []
+    for i, e in enumerate(eng):
+        mine = dests[i::K2]
+        ids = []
+        for d in mine:
+            rid, pid = topo.addr(d, core)
+            ids.append(DstId(rid=rid, pnc=pid))
+        transfers.append(RemoteDMATransfer(dst_ids=ids, dma_engine_mask=1 << e, remote_sem=T.sem.arr,
+                                           srcs=[T.relay[:]], dsts=[T.gath[r] for _ in mine], alu_op=0))
+    g.wait_ge(T.sem.harr, K1)
+    g.remote_dma_fused(transfers, local_sem=T.sem.hsent)
+    g.wait_ge(T.sem.hsent, K2)
+
+
+def rank_program(g, core, T, topo):
+    rank = T.rank_of(core)
+    if rank is None:
+        for r, c in enumerate(T.cores):
+            if _relay_of(c, T.cores, topo) == core:
+                _relay_program(g, core, T, topo, r)
+        return
+    S = T.sem
+    V, A, P, Q = g.vector, g.scalar, g.tensor, g.sync
+    Act = ActivationFunctionType
+    tk = T.x.shape[1]
+    nt = N * tk
+    half = tk // 2
+
+    Q.dma_start(T.xs[:], T.x[:]).then_inc(S.ld, 16)
+
+    V.memset(T.tab[0:KK, :], 1.0).then_inc(S.cst, 1)
+    V.memset(T.w[0:KK, :], 0.0).then_inc(S.cst, 1)
+    V.wait_ge(S.cst, 2)
+    V.memset(T.w[0:N, 0:N], -1.0 / N).then_inc(S.cst, 1)
+    V.memset(T.w[ROW_M2:ROW_M2 + N, N:N + 1], 1.0 / nt).then_inc(S.cst, 1)
+    V.memset(T.w[ROW_ONE:KK, N:N + 1], EPS).then_inc(S.cst, 1)
+    V.memset(T.w[0:N, N + 1:N + 2], 1.0 / N).then_inc(S.cst, 1)
+    g.wait_ge(S.cst, 6)
+    g.affine_select(T.w[0:N, 0:N], T.w[0:N, 0:N], [[-1, N]], AluOpType.not_equal, 1.0 - 1.0 / N, 0, 1).then_inc(S.diag, 1)
+
+    A.wait_ge(S.ld, 16)
+    A.activation(T.junk[:], T.xs[:], Act.Identity, scale=-1.0 / tk, accum_out=T.st[:, 0:1]).then_inc(S.a, 1)
+    A.wait_ge(S.a, 1)
+    A.activation(T.junk[:], T.xs[:], Act.Square, bias=T.st[:, 0:1], accum_out=T.st[:, 1:2]).then_inc(S.a, 1)
+
+    relay = _relay_of(core, T.cores, topo)
+    rid, pid = topo.addr(relay, core)
+    m1 = 0
+    for e in _bits(topo.mask(core, relay))[:K1]:
+        m1 |= 1 << e
+    g.wait_ge(S.a, 2)
+    g.remote_dma(T.relay[:], T.st[:], S.harr, S.sent, pid, rid, m1)
+
+    Q.wait_ge(S.cst, 6)
+    Q.wait_ge(S.arr, N)
+    Q.dma_start(T.tab[0:N, 1:2 * 128 + 1], T.gath[:]).then_inc(S.gl, 16)
+    A.wait_ge(S.cst, 6)
+    A.wait_ge(S.arr, N)
+    A.dma_start(T.tab[ROW_M2:ROW_M2 + N, 0:2 * 128], T.gath[:]).then_inc(S.gl, 16)
+
+    lhsT = T.tab[0:KK, 1:2 * 128 + 1:2]
+    P.wait_ge(S.cst, 6)
+    P.wait_ge(S.diag, 1)
+    P.wait_ge(S.gl, 32)
+    P.matmul(T.ps[:, 0:N + 1], lhsT, T.w[0:KK, 0:N + 1], True, True).then_inc(S.mm, 1)
+    P.matmul(T.ps2[:, 0:1], lhsT, T.w[0:KK, N + 1:N + 2], True, True).then_inc(S.mm2, 1)
+
+    V.wait_ge(S.ld, 16)
+    V.wait_ge(S.mm2, 1)
+    V.tensor_scalar(T.xm[:], T.xs[:], T.ps2[:, 0:1], None, AluOpType.add).then_inc(S.xmd, 1)
+
+    A.wait_ge(S.mm, 1)
+    A.activation(T.j10[:, 0:N], T.ps[:, 0:N], Act.Square, scale=math.sqrt(1.0 / N), accum_out=T.sc[:, 0:1]).then_inc(S.p, 1)
+    A.wait_ge(S.p, 1)
+    A.activation(T.sc[:, 1:2], T.ps[:, N:N + 1], Act.Sqrt, bias=T.sc[:, 0:1]).then_inc(S.p, 1)
+
+    V.wait_ge(S.p, 2)
+    V.reciprocal(T.sc[:, 2:3], T.sc[:, 1:2]).then_inc(S.r, 1)
+
+    V.wait_ge(S.r, 1)
+    V.wait_ge(S.xmd, 1)
+    V.tensor_scalar(T.ys[:, 0:half], T.xm[:, 0:half], T.sc[:, 2:3], None, AluOpType.mult).then_inc(S.y1, 1)
+    A.wait_ge(S.r, 1)
+    A.wait_ge(S.xmd, 1)
+    A.activation(T.ys[:, half:tk], T.xm[:, half:tk], Act.Identity, scale=T.sc[:, 2:3]).then_inc(S.y2, 1)
+
+    Q.wait_ge(S.y1, 1)
+    Q.wait_ge(S.y2, 1)
+    Q.dma_start(T.y[:], T.ys[:]).then_inc(S.stq, 16)
+    Q.wait_ge(S.stq, 16)
+    g.wait_ge(S.sent, K1)

@@ -25,8 +25,8 @@ SCRATCH = {
     "ps": ("psum", [128, 512], "float32"),
     "ps2": ("psum", [128, 512], "float32"),
 }
-SEMAPHORES = ["ld", "cst", "diag", "a", "harr", "sent", "hsent", "arr", "gl", "mm", "mm2", "p", "r", "xmd", "y1", "y2",
-              "stq"]
+SEMAPHORES = ["ld", "cst", "diag", "a", "harr", "sent", "hsent", "arr", "gl", "mm", "mm2", "p", "sv", "si", "xmd", "y1",
+              "y2", "stq"]
 
 
 def _bits(mask):
@@ -76,6 +76,7 @@ def rank_program(g, core, T, topo):
     tk = T.x.shape[1]
     nt = N * tk
     half = tk // 2
+    c_q, c_sd, c_v, c_iv = [T.sc[:, i:i + 1] for i in range(4)]
 
     Q.dma_start(T.xs[:], T.x[:]).then_inc(S.ld, 16)
 
@@ -114,26 +115,28 @@ def rank_program(g, core, T, topo):
     P.wait_ge(S.diag, 1)
     P.wait_ge(S.gl, 32)
     P.matmul(T.ps[:, 0:N + 1], lhsT, T.w[0:KK, 0:N + 1], True, True).then_inc(S.mm, 1)
-    P.matmul(T.ps2[:, 0:1], lhsT, T.w[0:KK, N + 1:N + 2], True, True).then_inc(S.mm2, 1)
-
-    V.wait_ge(S.ld, 16)
-    V.wait_ge(S.mm2, 1)
-    V.tensor_scalar(T.xm[:], T.xs[:], T.ps2[:, 0:1], None, AluOpType.add).then_inc(S.xmd, 1)
+    P.matmul(T.ps2[:, 0:2], lhsT, T.w[0:KK, N:N + 2], True, True).then_inc(S.mm2, 1)
 
     A.wait_ge(S.mm, 1)
-    A.activation(T.j10[:, 0:N], T.ps[:, 0:N], Act.Square, scale=math.sqrt(1.0 / N), accum_out=T.sc[:, 0:1]).then_inc(S.p, 1)
+    A.activation(T.j10[:, 0:N], T.ps[:, 0:N], Act.Square, scale=math.sqrt(1.0 / N), accum_out=c_q).then_inc(S.p, 1)
     A.wait_ge(S.p, 1)
-    A.activation(T.sc[:, 1:2], T.ps[:, N:N + 1], Act.Sqrt, bias=T.sc[:, 0:1]).then_inc(S.p, 1)
+    A.activation(c_sd, T.ps[:, N:N + 1], Act.Sqrt, bias=c_q).then_inc(S.p, 1)
 
-    V.wait_ge(S.p, 2)
-    V.reciprocal(T.sc[:, 2:3], T.sc[:, 1:2]).then_inc(S.r, 1)
+    V.wait_ge(S.mm2, 1)
+    V.wait_ge(S.p, 1)
+    V.tensor_scalar(c_v, c_q, T.ps2[:, 0:1], None, AluOpType.add).then_inc(S.sv, 1)
+    V.wait_ge(S.sv, 1)
+    V.reciprocal(c_iv, c_v).then_inc(S.si, 1)
+    V.wait_ge(S.si, 1)
+    V.wait_ge(S.ld, 16)
+    V.tensor_scalar(T.xm[:], T.xs[:], T.ps2[:, 1:2], c_iv, AluOpType.add, AluOpType.mult).then_inc(S.xmd, 1)
 
-    V.wait_ge(S.r, 1)
     V.wait_ge(S.xmd, 1)
-    V.tensor_scalar(T.ys[:, 0:half], T.xm[:, 0:half], T.sc[:, 2:3], None, AluOpType.mult).then_inc(S.y1, 1)
-    A.wait_ge(S.r, 1)
+    V.wait_ge(S.p, 2)
+    V.tensor_scalar(T.ys[:, 0:half], T.xm[:, 0:half], c_sd, None, AluOpType.mult).then_inc(S.y1, 1)
+    A.wait_ge(S.p, 2)
     A.wait_ge(S.xmd, 1)
-    A.activation(T.ys[:, half:tk], T.xm[:, half:tk], Act.Identity, scale=T.sc[:, 2:3]).then_inc(S.y2, 1)
+    A.activation(T.ys[:, half:tk], T.xm[:, half:tk], Act.Identity, scale=c_sd).then_inc(S.y2, 1)
 
     Q.wait_ge(S.y1, 1)
     Q.wait_ge(S.y2, 1)

@@ -5,9 +5,8 @@ from concourse.mybir import AluOpType, ActivationFunctionType
 N = 10
 EPS = 0.01
 K1 = 8
-K2 = 4
-ROW_M2 = 32
-ROW_ONE = 64
+K2 = 2
+ROW_ONE = 32
 KK = ROW_ONE + 1
 
 SCRATCH = {
@@ -16,21 +15,34 @@ SCRATCH = {
     "ys": ("sbuf", [128, 256], "float32"),
     "junk": ("sbuf", [128, 256], "float32"),
     "j10": ("sbuf", [128, 16], "float32"),
-    "st": ("sbuf", [128, 2], "float32"),
+    "st": ("sbuf", [128, 8], "float32"),
     "sc": ("sbuf", [128, 4], "float32"),
-    "tab": ("sbuf", [128, 260], "float32"),
-    "w": ("sbuf", [128, 12], "float32"),
-    "relay": ("dram", [128, 2], "float32"),
-    "gath": ("dram", [N, 128, 2], "float32"),
-    "ps": ("psum", [128, 512], "float32"),
+    "taba": ("sbuf", [128, 128], "float32"),
+    "tabb": ("sbuf", [128, 128], "float32"),
+    "wa": ("sbuf", [128, 12], "float32"),
+    "wb": ("sbuf", [128, 4], "float32"),
+    "rla": ("dram", [128, 1], "float32"),
+    "rlb": ("dram", [128, 1], "float32"),
+    "gatha": ("dram", [N, 128, 1], "float32"),
+    "gathb": ("dram", [N, 128, 1], "float32"),
+    "ps0": ("psum", [128, 512], "float32"),
+    "ps1": ("psum", [128, 512], "float32"),
     "ps2": ("psum", [128, 512], "float32"),
+    "ps3": ("psum", [128, 512], "float32"),
 }
-SEMAPHORES = ["ld", "cst", "diag", "a", "harr", "sent", "hsent", "arr", "gl", "mm", "mm2", "p", "sv", "si", "xmd", "y1",
-              "y2", "stq"]
+SEMAPHORES = ["ld", "cst", "diag", "a", "harra", "harrb", "sent", "hsent", "arra", "arrb", "gla", "glb", "mmd", "mmn",
+              "mmv", "mmw", "p", "sv", "si", "xmd", "y1", "y2", "stq"]
 
 
 def _bits(mask):
     return [b for b in range(mask.bit_length()) if (mask >> b) & 1]
+
+
+def _mask_of(bits):
+    m = 0
+    for b in bits:
+        m |= 1 << b
+    return m
 
 
 def _relay_of(rank_core, cores, topo):
@@ -43,24 +55,27 @@ def _relay_of(rank_core, cores, topo):
 
 
 def _relay_program(g, core, T, topo, r):
+    S = T.sem
     dests = list(T.cores)
     common = topo.mask(core, dests[0])
     for d in dests:
         common &= topo.mask(core, d)
     eng = _bits(common)
-    eng = eng[::len(eng) // K2][:K2]
-    transfers = []
-    for i, e in enumerate(eng):
-        mine = dests[i::K2]
-        ids = []
-        for d in mine:
-            rid, pid = topo.addr(d, core)
-            ids.append(DstId(rid=rid, pnc=pid))
-        transfers.append(RemoteDMATransfer(dst_ids=ids, dma_engine_mask=1 << e, remote_sem=T.sem.arr,
-                                           srcs=[T.relay[:]], dsts=[T.gath[r] for _ in mine], alu_op=0))
-    g.wait_ge(T.sem.harr, K1)
-    g.remote_dma_fused(transfers, local_sem=T.sem.hsent)
-    g.wait_ge(T.sem.hsent, K2)
+    eng = eng[::len(eng) // (2 * K2)][:2 * K2]
+    for which, (src, dst, landed, there) in enumerate(((T.rla[:], T.gatha[r], S.harra, S.arra),
+                                                       (T.rlb[:], T.gathb[r], S.harrb, S.arrb))):
+        transfers = []
+        for i, e in enumerate(eng[which * K2:(which + 1) * K2]):
+            mine = dests[i::K2]
+            ids = []
+            for d in mine:
+                rid, pid = topo.addr(d, core)
+                ids.append(DstId(rid=rid, pnc=pid))
+            transfers.append(RemoteDMATransfer(dst_ids=ids, dma_engine_mask=1 << e, remote_sem=there,
+                                               srcs=[src], dsts=[dst for _ in mine], alu_op=0))
+        g.wait_ge(landed, K1)
+        g.remote_dma_fused(transfers, local_sem=S.hsent)
+    g.wait_ge(S.hsent, 2 * K2)
 
 
 def rank_program(g, core, T, topo):
@@ -80,56 +95,59 @@ def rank_program(g, core, T, topo):
 
     Q.dma_start(T.xs[:], T.x[:]).then_inc(S.ld, 16)
 
-    V.memset(T.tab[0:KK, :], 1.0).then_inc(S.cst, 1)
-    V.memset(T.w[0:KK, :], 0.0).then_inc(S.cst, 1)
+    V.memset(T.tabb[0:KK, :], 1.0).then_inc(S.cst, 1)
+    V.memset(T.wb[0:KK, 0:1], 0.0).then_inc(S.cst, 1)
     V.wait_ge(S.cst, 2)
-    V.memset(T.w[0:N, 0:N], -1.0 / N).then_inc(S.cst, 1)
-    V.memset(T.w[ROW_M2:ROW_M2 + N, N:N + 1], 1.0 / nt).then_inc(S.cst, 1)
-    V.memset(T.w[ROW_ONE:KK, N:N + 1], EPS).then_inc(S.cst, 1)
-    V.memset(T.w[0:N, N + 1:N + 2], 1.0 / N).then_inc(S.cst, 1)
+    V.memset(T.wb[0:N, 0:1], 1.0 / nt).then_inc(S.cst, 1)
+    V.memset(T.wb[ROW_ONE:KK, 0:1], EPS).then_inc(S.cst, 1)
+    V.memset(T.wa[0:N, 0:N], -1.0 / N).then_inc(S.cst, 1)
+    V.memset(T.wa[0:N, N:N + 1], 1.0 / N).then_inc(S.cst, 1)
     g.wait_ge(S.cst, 6)
-    g.affine_select(T.w[0:N, 0:N], T.w[0:N, 0:N], [[-1, N]], AluOpType.not_equal, 1.0 - 1.0 / N, 0, 1).then_inc(S.diag, 1)
+    g.affine_select(T.wa[0:N, 0:N], T.wa[0:N, 0:N], [[-1, N]], AluOpType.not_equal, 1.0 - 1.0 / N, 0, 1).then_inc(S.diag, 1)
 
     A.wait_ge(S.ld, 16)
     A.activation(T.junk[:], T.xs[:], Act.Identity, scale=-1.0 / tk, accum_out=T.st[:, 0:1]).then_inc(S.a, 1)
     A.wait_ge(S.a, 1)
-    A.activation(T.junk[:], T.xs[:], Act.Square, bias=T.st[:, 0:1], accum_out=T.st[:, 1:2]).then_inc(S.a, 1)
+    A.activation(T.junk[:], T.xs[:], Act.Square, bias=T.st[:, 0:1], accum_out=T.st[:, 4:5]).then_inc(S.a, 1)
 
     relay = _relay_of(core, T.cores, topo)
     rid, pid = topo.addr(relay, core)
-    m1 = 0
-    for e in _bits(topo.mask(core, relay))[:K1]:
-        m1 |= 1 << e
+    eng = _bits(topo.mask(core, relay))
+    g.wait_ge(S.a, 1)
+    g.remote_dma(T.rla[:], T.st[:, 0:1], S.harra, S.sent, pid, rid, _mask_of(eng[0:K1]))
     g.wait_ge(S.a, 2)
-    g.remote_dma(T.relay[:], T.st[:], S.harr, S.sent, pid, rid, m1)
+    g.remote_dma(T.rlb[:], T.st[:, 4:5], S.harrb, S.sent, pid, rid, _mask_of(eng[K1:2 * K1]))
 
     Q.wait_ge(S.cst, 6)
-    Q.wait_ge(S.arr, N)
-    Q.dma_start(T.tab[0:N, 1:2 * 128 + 1], T.gath[:]).then_inc(S.gl, 16)
-    A.wait_ge(S.cst, 6)
-    A.wait_ge(S.arr, N)
-    A.dma_start(T.tab[ROW_M2:ROW_M2 + N, 0:2 * 128], T.gath[:]).then_inc(S.gl, 16)
+    Q.wait_ge(S.arra, N)
+    Q.dma_start(T.taba[0:N, :], T.gatha[:]).then_inc(S.gla, 16)
+    Q.wait_ge(S.arrb, N)
+    Q.dma_start(T.tabb[0:N, :], T.gathb[:]).then_inc(S.glb, 16)
 
-    lhsT = T.tab[0:KK, 1:2 * 128 + 1:2]
     P.wait_ge(S.cst, 6)
     P.wait_ge(S.diag, 1)
-    P.wait_ge(S.gl, 32)
-    P.matmul(T.ps[:, 0:N + 1], lhsT, T.w[0:KK, 0:N + 1], True, True).then_inc(S.mm, 1)
-    P.matmul(T.ps2[:, 0:2], lhsT, T.w[0:KK, N:N + 2], True, True).then_inc(S.mm2, 1)
+    P.wait_ge(S.gla, 16)
+    P.matmul(T.ps0[:, 0:N], T.taba[0:N, :], T.wa[0:N, 0:N], True, True).then_inc(S.mmd, 1)
+    P.matmul(T.ps1[:, 0:1], T.taba[0:N, :], T.wa[0:N, N:N + 1], True, True).then_inc(S.mmn, 1)
+    P.wait_ge(S.glb, 16)
+    P.matmul(T.ps2[:, 0:1], T.tabb[0:KK, :], T.wb[0:KK, 0:1], True, True).then_inc(S.mmv, 1)
+    P.matmul(T.ps3[:, 0:1], T.tabb[0:KK, :], T.wb[0:KK, 0:1], True, True).then_inc(S.mmw, 1)
 
-    A.wait_ge(S.mm, 1)
-    A.activation(T.j10[:, 0:N], T.ps[:, 0:N], Act.Square, scale=math.sqrt(1.0 / N), accum_out=c_q).then_inc(S.p, 1)
+    A.wait_ge(S.mmd, 1)
+    A.activation(T.j10[:, 0:N], T.ps0[:, 0:N], Act.Square, scale=math.sqrt(1.0 / N), accum_out=c_q).then_inc(S.p, 1)
     A.wait_ge(S.p, 1)
-    A.activation(c_sd, T.ps[:, N:N + 1], Act.Sqrt, bias=c_q).then_inc(S.p, 1)
+    A.wait_ge(S.mmv, 1)
+    A.activation(c_sd, T.ps2[:, 0:1], Act.Sqrt, bias=c_q).then_inc(S.p, 1)
 
-    V.wait_ge(S.mm2, 1)
     V.wait_ge(S.p, 1)
-    V.tensor_scalar(c_v, c_q, T.ps2[:, 0:1], None, AluOpType.add).then_inc(S.sv, 1)
+    V.wait_ge(S.mmw, 1)
+    V.tensor_scalar(c_v, c_q, T.ps3[:, 0:1], None, AluOpType.add).then_inc(S.sv, 1)
     V.wait_ge(S.sv, 1)
     V.reciprocal(c_iv, c_v).then_inc(S.si, 1)
     V.wait_ge(S.si, 1)
+    V.wait_ge(S.mmn, 1)
     V.wait_ge(S.ld, 16)
-    V.tensor_scalar(T.xm[:], T.xs[:], T.ps2[:, 1:2], c_iv, AluOpType.add, AluOpType.mult).then_inc(S.xmd, 1)
+    V.tensor_scalar(T.xm[:], T.xs[:], T.ps1[:, 0:1], c_iv, AluOpType.add, AluOpType.mult).then_inc(S.xmd, 1)
 
     V.wait_ge(S.xmd, 1)
     V.wait_ge(S.p, 2)
@@ -142,4 +160,4 @@ def rank_program(g, core, T, topo):
     Q.wait_ge(S.y2, 1)
     Q.dma_start(T.y[:], T.ys[:]).then_inc(S.stq, 16)
     Q.wait_ge(S.stq, 16)
-    g.wait_ge(S.sent, K1)
+    g.wait_ge(S.sent, 2 * K1)

@@ -16,7 +16,7 @@ SCRATCH = {
     "junk": ("sbuf", [128, 256], "float32"),
     "j10": ("sbuf", [128, 16], "float32"),
     "st": ("sbuf", [128, 8], "float32"),
-    "sc": ("sbuf", [128, 4], "float32"),
+    "sc": ("sbuf", [128, 8], "float32"),
     "taba": ("sbuf", [128, 128], "float32"),
     "tabb": ("sbuf", [128, 128], "float32"),
     "wa": ("sbuf", [128, 12], "float32"),
@@ -28,10 +28,9 @@ SCRATCH = {
     "ps0": ("psum", [128, 512], "float32"),
     "ps1": ("psum", [128, 512], "float32"),
     "ps2": ("psum", [128, 512], "float32"),
-    "ps3": ("psum", [128, 512], "float32"),
 }
 SEMAPHORES = ["ld", "cst", "diag", "a", "harra", "harrb", "sent", "hsent", "arra", "arrb", "gla", "glb", "mmd", "mmn",
-              "mmv", "mmw", "p", "sv", "si", "xmd", "y1", "y2", "stq"]
+              "mmv", "e", "p", "si", "xmd", "y1", "y2", "stq"]
 
 
 def _bits(mask):
@@ -91,7 +90,7 @@ def rank_program(g, core, T, topo):
     tk = T.x.shape[1]
     nt = N * tk
     half = tk // 2
-    c_q, c_sd, c_v, c_iv = [T.sc[:, i:i + 1] for i in range(4)]
+    c_c, c_ic, c_ic2, c_sn, c_q, c_s, c_r = [T.sc[:, i:i + 1] for i in range(7)]
 
     Q.dma_start(T.xs[:], T.x[:]).then_inc(S.ld, 16)
 
@@ -118,6 +117,14 @@ def rank_program(g, core, T, topo):
     g.wait_ge(S.a, 2)
     g.remote_dma(T.rlb[:], T.st[:, 4:5], S.harrb, S.sent, pid, rid, _mask_of(eng[K1:2 * K1]))
 
+    A.wait_ge(S.a, 2)
+    A.activation(c_c, T.st[:, 4:5], Act.Sqrt, bias=EPS, scale=1.0 / tk).then_inc(S.e, 1)
+    V.wait_ge(S.e, 1)
+    V.reciprocal(c_ic, c_c).then_inc(S.e, 1)
+    V.wait_ge(S.e, 2)
+    V.tensor_scalar(c_ic2, c_ic, c_ic, None, AluOpType.mult).then_inc(S.e, 1)
+    V.tensor_scalar(c_sn, c_ic, math.sqrt(1.0 / N), None, AluOpType.mult).then_inc(S.e, 1)
+
     Q.wait_ge(S.cst, 6)
     Q.wait_ge(S.arra, N)
     Q.dma_start(T.taba[0:N, :], T.gatha[:]).then_inc(S.gla, 16)
@@ -131,30 +138,27 @@ def rank_program(g, core, T, topo):
     P.matmul(T.ps1[:, 0:1], T.taba[0:N, :], T.wa[0:N, N:N + 1], True, True).then_inc(S.mmn, 1)
     P.wait_ge(S.glb, 16)
     P.matmul(T.ps2[:, 0:1], T.tabb[0:KK, :], T.wb[0:KK, 0:1], True, True).then_inc(S.mmv, 1)
-    P.matmul(T.ps3[:, 0:1], T.tabb[0:KK, :], T.wb[0:KK, 0:1], True, True).then_inc(S.mmw, 1)
 
+    A.wait_ge(S.e, 4)
     A.wait_ge(S.mmd, 1)
-    A.activation(T.j10[:, 0:N], T.ps0[:, 0:N], Act.Square, scale=math.sqrt(1.0 / N), accum_out=c_q).then_inc(S.p, 1)
-    A.wait_ge(S.p, 1)
-    A.wait_ge(S.mmv, 1)
-    A.activation(c_sd, T.ps2[:, 0:1], Act.Sqrt, bias=c_q).then_inc(S.p, 1)
-
-    V.wait_ge(S.p, 1)
-    V.wait_ge(S.mmw, 1)
-    V.tensor_scalar(c_v, c_q, T.ps3[:, 0:1], None, AluOpType.add).then_inc(S.sv, 1)
-    V.wait_ge(S.sv, 1)
-    V.reciprocal(c_iv, c_v).then_inc(S.si, 1)
-    V.wait_ge(S.si, 1)
+    A.activation(T.j10[:, 0:N], T.ps0[:, 0:N], Act.Square, scale=c_sn, accum_out=c_q).then_inc(S.p, 1)
+    V.wait_ge(S.e, 4)
     V.wait_ge(S.mmn, 1)
     V.wait_ge(S.ld, 16)
-    V.tensor_scalar(T.xm[:], T.xs[:], T.ps1[:, 0:1], c_iv, AluOpType.add, AluOpType.mult).then_inc(S.xmd, 1)
+    V.tensor_scalar(T.xm[:], T.xs[:], T.ps1[:, 0:1], c_ic, AluOpType.add, AluOpType.mult).then_inc(S.xmd, 1)
 
+    A.wait_ge(S.p, 1)
+    A.wait_ge(S.mmv, 1)
+    A.activation(c_s, T.ps2[:, 0:1], Act.Sqrt, bias=c_q, scale=c_ic2).then_inc(S.p, 1)
     V.wait_ge(S.xmd, 1)
     V.wait_ge(S.p, 2)
-    V.tensor_scalar(T.ys[:, 0:half], T.xm[:, 0:half], c_sd, None, AluOpType.mult).then_inc(S.y1, 1)
-    A.wait_ge(S.p, 2)
+    V.reciprocal(c_r, c_s).then_inc(S.si, 1)
+
+    V.wait_ge(S.si, 1)
+    V.tensor_scalar(T.ys[:, 0:half], T.xm[:, 0:half], c_r, None, AluOpType.mult).then_inc(S.y1, 1)
+    A.wait_ge(S.si, 1)
     A.wait_ge(S.xmd, 1)
-    A.activation(T.ys[:, half:tk], T.xm[:, half:tk], Act.Identity, scale=c_sd).then_inc(S.y2, 1)
+    A.activation(T.ys[:, half:tk], T.xm[:, half:tk], Act.Identity, scale=c_r).then_inc(S.y2, 1)
 
     Q.wait_ge(S.y1, 1)
     Q.wait_ge(S.y2, 1)

@@ -6,31 +6,35 @@ N = 10
 EPS = 0.01
 K1 = 8
 K2 = 2
-ROW_ONE = 32
-KK = ROW_ONE + 1
+ROW2 = 32
+KA = ROW2 + N
+KB = ROW2 + 1
 
 SCRATCH = {
+    "xh": ("sbuf", [128, 2], "float32"),
     "xs": ("sbuf", [128, 256], "float32"),
     "xm": ("sbuf", [128, 256], "float32"),
     "ys": ("sbuf", [128, 256], "float32"),
     "junk": ("sbuf", [128, 256], "float32"),
-    "j10": ("sbuf", [128, 16], "float32"),
+    "j20": ("sbuf", [128, 24], "float32"),
     "st": ("sbuf", [128, 8], "float32"),
     "sc": ("sbuf", [128, 8], "float32"),
     "taba": ("sbuf", [128, 128], "float32"),
     "tabb": ("sbuf", [128, 128], "float32"),
-    "wa": ("sbuf", [128, 12], "float32"),
+    "wa": ("sbuf", [128, 24], "float32"),
     "wb": ("sbuf", [128, 4], "float32"),
+    "rl0": ("dram", [128, 1], "float32"),
     "rla": ("dram", [128, 1], "float32"),
     "rlb": ("dram", [128, 1], "float32"),
+    "gath0": ("dram", [N, 128, 1], "float32"),
     "gatha": ("dram", [N, 128, 1], "float32"),
     "gathb": ("dram", [N, 128, 1], "float32"),
     "ps0": ("psum", [128, 512], "float32"),
     "ps1": ("psum", [128, 512], "float32"),
     "ps2": ("psum", [128, 512], "float32"),
 }
-SEMAPHORES = ["ld", "cst", "diag", "a", "harra", "harrb", "sent", "hsent", "arra", "arrb", "gla", "glb", "mmd", "mmn",
-              "mmv", "e", "p", "si", "xmd", "y1", "y2", "stq"]
+SEMAPHORES = ["ldh", "ld", "cst", "diag", "a", "harr0", "harra", "harrb", "sent", "hsent", "arr0", "arra", "arrb",
+              "gl0", "gla", "glb", "mmd", "mmn", "mmv", "e", "p", "si", "xmd", "y1", "y2", "stq"]
 
 
 def _bits(mask):
@@ -61,10 +65,12 @@ def _relay_program(g, core, T, topo, r):
         common &= topo.mask(core, d)
     eng = _bits(common)
     eng = eng[::len(eng) // (2 * K2)][:2 * K2]
-    for which, (src, dst, landed, there) in enumerate(((T.rla[:], T.gatha[r], S.harra, S.arra),
-                                                       (T.rlb[:], T.gathb[r], S.harrb, S.arrb))):
+    streams = ((T.rl0[:], T.gath0[r], S.harr0, S.arr0, eng[0:K2]),
+               (T.rla[:], T.gatha[r], S.harra, S.arra, eng[0:K2]),
+               (T.rlb[:], T.gathb[r], S.harrb, S.arrb, eng[K2:2 * K2]))
+    for src, dst, landed, there, engines in streams:
         transfers = []
-        for i, e in enumerate(eng[which * K2:(which + 1) * K2]):
+        for i, e in enumerate(engines):
             mine = dests[i::K2]
             ids = []
             for d in mine:
@@ -74,7 +80,7 @@ def _relay_program(g, core, T, topo, r):
                                                srcs=[src], dsts=[dst for _ in mine], alu_op=0))
         g.wait_ge(landed, K1)
         g.remote_dma_fused(transfers, local_sem=S.hsent)
-    g.wait_ge(S.hsent, 2 * K2)
+    g.wait_ge(S.hsent, len(streams) * K2)
 
 
 def rank_program(g, core, T, topo):
@@ -90,32 +96,46 @@ def rank_program(g, core, T, topo):
     tk = T.x.shape[1]
     nt = N * tk
     half = tk // 2
-    c_c, c_ic, c_ic2, c_sn, c_q, c_s, c_r = [T.sc[:, i:i + 1] for i in range(7)]
+    c_c, c_ic, c_ic2, c_q, c_s, c_r = [T.sc[:, i:i + 1] for i in range(6)]
+    w1, w2 = 1.0 / nt, (tk - 1.0) / nt
+    a1, a2 = math.sqrt(w1), math.sqrt(w2)
 
+    Q.dma_start(T.xh[:], T.x[:, 0:2]).then_inc(S.ldh, 16)
     Q.dma_start(T.xs[:], T.x[:]).then_inc(S.ld, 16)
 
-    V.memset(T.tabb[0:KK, :], 1.0).then_inc(S.cst, 1)
-    V.memset(T.wb[0:KK, 0:1], 0.0).then_inc(S.cst, 1)
-    V.wait_ge(S.cst, 2)
+    V.memset(T.tabb[0:KB, :], 1.0).then_inc(S.cst, 1)
+    V.memset(T.wb[0:KB, 0:1], 0.0).then_inc(S.cst, 1)
+    V.memset(T.taba[0:KA, :], 0.0).then_inc(S.cst, 1)
+    V.memset(T.wa[0:KA, 0:2 * N + 1], 0.0).then_inc(S.cst, 1)
+    V.wait_ge(S.cst, 4)
     V.memset(T.wb[0:N, 0:1], 1.0 / nt).then_inc(S.cst, 1)
-    V.memset(T.wb[ROW_ONE:KK, 0:1], EPS).then_inc(S.cst, 1)
-    V.memset(T.wa[0:N, 0:N], -1.0 / N).then_inc(S.cst, 1)
-    V.memset(T.wa[0:N, N:N + 1], 1.0 / N).then_inc(S.cst, 1)
-    g.wait_ge(S.cst, 6)
-    g.affine_select(T.wa[0:N, 0:N], T.wa[0:N, 0:N], [[-1, N]], AluOpType.not_equal, 1.0 - 1.0 / N, 0, 1).then_inc(S.diag, 1)
+    V.memset(T.wb[ROW2:KB, 0:1], EPS).then_inc(S.cst, 1)
+    V.memset(T.wa[0:N, 0:N], -a1 * w1).then_inc(S.cst, 1)
+    V.memset(T.wa[0:N, N:2 * N], -a2 * w1).then_inc(S.cst, 1)
+    V.memset(T.wa[0:N, 2 * N:2 * N + 1], -w1).then_inc(S.cst, 1)
+    V.memset(T.wa[ROW2:KA, 0:N], a1 * w2).then_inc(S.cst, 1)
+    V.memset(T.wa[ROW2:KA, N:2 * N], a2 * w2).then_inc(S.cst, 1)
+    V.memset(T.wa[ROW2:KA, 2 * N:2 * N + 1], w2).then_inc(S.cst, 1)
+    NCST = 12
 
     A.wait_ge(S.ld, 16)
-    A.activation(T.junk[:], T.xs[:], Act.Identity, scale=-1.0 / tk, accum_out=T.st[:, 0:1]).then_inc(S.a, 1)
+    A.activation(T.junk[:, 1:tk], T.xs[:, 1:tk], Act.Identity, scale=-1.0 / (tk - 1), accum_out=T.st[:, 0:1]).then_inc(S.a, 1)
     A.wait_ge(S.a, 1)
-    A.activation(T.junk[:], T.xs[:], Act.Square, bias=T.st[:, 0:1], accum_out=T.st[:, 4:5]).then_inc(S.a, 1)
+    A.activation(T.junk[:, 1:tk], T.xs[:, 1:tk], Act.Square, bias=T.st[:, 0:1], accum_out=T.st[:, 4:5]).then_inc(S.a, 1)
 
     relay = _relay_of(core, T.cores, topo)
     rid, pid = topo.addr(relay, core)
-    eng = _bits(topo.mask(core, relay))
+    m1 = _mask_of(_bits(topo.mask(core, relay))[0:K1])
+    g.wait_ge(S.ldh, 16)
+    g.remote_dma(T.rl0[:], T.xh[:, 0:1], S.harr0, S.sent, pid, rid, m1)
     g.wait_ge(S.a, 1)
-    g.remote_dma(T.rla[:], T.st[:, 0:1], S.harra, S.sent, pid, rid, _mask_of(eng[0:K1]))
+    g.remote_dma(T.rla[:], T.st[:, 0:1], S.harra, S.sent, pid, rid, m1)
     g.wait_ge(S.a, 2)
-    g.remote_dma(T.rlb[:], T.st[:, 4:5], S.harrb, S.sent, pid, rid, _mask_of(eng[K1:2 * K1]))
+    g.remote_dma(T.rlb[:], T.st[:, 4:5], S.harrb, S.sent, pid, rid, m1)
+    g.wait_ge(S.cst, NCST)
+    g.affine_select(T.wa[0:N, 0:N], T.wa[0:N, 0:N], [[-1, N]], AluOpType.not_equal, a1 * (1.0 - w1), 0, 1).then_inc(S.diag, 1)
+    g.affine_select(T.wa[ROW2:KA, N:2 * N], T.wa[ROW2:KA, N:2 * N], [[-1, N]], AluOpType.not_equal, -a2 * (1.0 - w2), 0,
+                    1).then_inc(S.diag, 1)
 
     A.wait_ge(S.a, 2)
     A.activation(c_c, T.st[:, 4:5], Act.Sqrt, bias=EPS, scale=1.0 / tk).then_inc(S.e, 1)
@@ -123,26 +143,29 @@ def rank_program(g, core, T, topo):
     V.reciprocal(c_ic, c_c).then_inc(S.e, 1)
     V.wait_ge(S.e, 2)
     V.tensor_scalar(c_ic2, c_ic, c_ic, None, AluOpType.mult).then_inc(S.e, 1)
-    V.tensor_scalar(c_sn, c_ic, math.sqrt(1.0 / N), None, AluOpType.mult).then_inc(S.e, 1)
 
-    Q.wait_ge(S.cst, 6)
+    A.wait_ge(S.cst, NCST)
+    A.wait_ge(S.arr0, N)
+    A.dma_start(T.taba[0:N, :], T.gath0[:]).then_inc(S.gl0, 16)
+    Q.wait_ge(S.cst, NCST)
     Q.wait_ge(S.arra, N)
-    Q.dma_start(T.taba[0:N, :], T.gatha[:]).then_inc(S.gla, 16)
+    Q.dma_start(T.taba[ROW2:KA, :], T.gatha[:]).then_inc(S.gla, 16)
     Q.wait_ge(S.arrb, N)
     Q.dma_start(T.tabb[0:N, :], T.gathb[:]).then_inc(S.glb, 16)
 
-    P.wait_ge(S.cst, 6)
-    P.wait_ge(S.diag, 1)
+    P.wait_ge(S.cst, NCST)
+    P.wait_ge(S.diag, 2)
+    P.wait_ge(S.gl0, 16)
     P.wait_ge(S.gla, 16)
-    P.matmul(T.ps0[:, 0:N], T.taba[0:N, :], T.wa[0:N, 0:N], True, True).then_inc(S.mmd, 1)
-    P.matmul(T.ps1[:, 0:1], T.taba[0:N, :], T.wa[0:N, N:N + 1], True, True).then_inc(S.mmn, 1)
+    P.matmul(T.ps0[:, 0:2 * N], T.taba[0:KA, :], T.wa[0:KA, 0:2 * N], True, True).then_inc(S.mmd, 1)
+    P.matmul(T.ps1[:, 0:1], T.taba[0:KA, :], T.wa[0:KA, 2 * N:2 * N + 1], True, True).then_inc(S.mmn, 1)
     P.wait_ge(S.glb, 16)
-    P.matmul(T.ps2[:, 0:1], T.tabb[0:KK, :], T.wb[0:KK, 0:1], True, True).then_inc(S.mmv, 1)
+    P.matmul(T.ps2[:, 0:1], T.tabb[0:KB, :], T.wb[0:KB, 0:1], True, True).then_inc(S.mmv, 1)
 
-    A.wait_ge(S.e, 4)
+    A.wait_ge(S.e, 3)
     A.wait_ge(S.mmd, 1)
-    A.activation(T.j10[:, 0:N], T.ps0[:, 0:N], Act.Square, scale=c_sn, accum_out=c_q).then_inc(S.p, 1)
-    V.wait_ge(S.e, 4)
+    A.activation(T.j20[:, 0:2 * N], T.ps0[:, 0:2 * N], Act.Square, scale=c_ic, accum_out=c_q).then_inc(S.p, 1)
+    V.wait_ge(S.e, 3)
     V.wait_ge(S.mmn, 1)
     V.wait_ge(S.ld, 16)
     V.tensor_scalar(T.xm[:], T.xs[:], T.ps1[:, 0:1], c_ic, AluOpType.add, AluOpType.mult).then_inc(S.xmd, 1)
@@ -164,4 +187,4 @@ def rank_program(g, core, T, topo):
     Q.wait_ge(S.y2, 1)
     Q.dma_start(T.y[:], T.ys[:]).then_inc(S.stq, 16)
     Q.wait_ge(S.stq, 16)
-    g.wait_ge(S.sent, 2 * K1)
+    g.wait_ge(S.sent, 3 * K1)

@@ -3,12 +3,17 @@ from concourse.bass import DstId, RemoteDMATransfer
 from concourse.mybir import AluOpType, ActivationFunctionType
 
 N = 10
+TK = 256
+NT = N * TK
 EPS = 0.01
+W1, W2 = 1.0 / NT, (TK - 1.0) / NT
+A1, A2 = math.sqrt(W1), math.sqrt(W2)
 K1 = 8
 K2 = 2
 ROW2 = 32
 KA = ROW2 + N
 KB = ROW2 + 1
+CB = 24
 
 SCRATCH = {
     "xh": ("sbuf", [128, 2], "float32"),
@@ -21,8 +26,7 @@ SCRATCH = {
     "sc": ("sbuf", [128, 8], "float32"),
     "taba": ("sbuf", [128, 128], "float32"),
     "tabb": ("sbuf", [128, 128], "float32"),
-    "wa": ("sbuf", [128, 24], "float32"),
-    "wb": ("sbuf", [128, 4], "float32"),
+    "wc": ("sbuf", [128, 28], "float32"),
     "rl0": ("dram", [128, 1], "float32"),
     "rla": ("dram", [128, 1], "float32"),
     "rlb": ("dram", [128, 1], "float32"),
@@ -33,8 +37,8 @@ SCRATCH = {
     "ps1": ("psum", [128, 512], "float32"),
     "ps2": ("psum", [128, 512], "float32"),
 }
-SEMAPHORES = ["ldh", "ld", "cst", "diag", "a", "harr0", "harra", "harrb", "sent", "hsent", "arr0", "arra", "arrb",
-              "gl0", "gla", "glb", "mmd", "mmn", "mmv", "e", "p", "si", "xmd", "y1", "y2", "stq"]
+SEMAPHORES = ["ldh", "ld", "cst", "cs2", "diag", "carr", "a", "harr0", "harra", "harrb", "sent", "hsent", "arr0", "arra",
+              "arrb", "gl0", "gla", "glb", "mmd", "mmn", "mmv", "e", "p", "si", "xmd", "y1", "y2", "stq"]
 
 
 def _bits(mask):
@@ -59,12 +63,33 @@ def _relay_of(rank_core, cores, topo):
 
 def _relay_program(g, core, T, topo, r):
     S = T.sem
+    V = g.vector
     dests = list(T.cores)
     common = topo.mask(core, dests[0])
     for d in dests:
         common &= topo.mask(core, d)
     eng = _bits(common)
     eng = eng[::len(eng) // (2 * K2)][:2 * K2]
+
+    V.memset(T.wc[:], 0.0).then_inc(S.cst, 1)
+    V.wait_ge(S.cst, 1)
+    V.memset(T.wc[0:N, 0:N], -A1 * W1).then_inc(S.cst, 1)
+    V.memset(T.wc[ROW2:KA, N:2 * N], A2 * W2).then_inc(S.cst, 1)
+    V.memset(T.wc[0:N, N:2 * N], -A2 * W1).then_inc(S.cs2, 1)
+    V.memset(T.wc[ROW2:KA, 0:N], A1 * W2).then_inc(S.cs2, 1)
+    V.memset(T.wc[0:N, 2 * N:2 * N + 1], -W1).then_inc(S.cs2, 1)
+    V.memset(T.wc[ROW2:KA, 2 * N:2 * N + 1], W2).then_inc(S.cs2, 1)
+    V.memset(T.wc[0:N, CB:CB + 1], 1.0 / NT).then_inc(S.cs2, 1)
+    V.memset(T.wc[ROW2:KB, CB:CB + 1], EPS).then_inc(S.cs2, 1)
+    g.wait_ge(S.cst, 3)
+    g.affine_select(T.wc[0:N, 0:N], T.wc[0:N, 0:N], [[-1, N]], AluOpType.not_equal, A1 * (1.0 - W1), 0, 1).then_inc(S.diag, 1)
+    g.affine_select(T.wc[ROW2:KA, N:2 * N], T.wc[ROW2:KA, N:2 * N], [[-1, N]], AluOpType.not_equal, -A2 * (1.0 - W2), 0,
+                    1).then_inc(S.diag, 1)
+    g.wait_ge(S.cs2, 6)
+    g.wait_ge(S.diag, 2)
+    rid, pid = topo.addr(T.cores[r], core)
+    g.remote_dma(T.wc[:], T.wc[:], S.carr, S.hsent, pid, rid, _mask_of(eng))
+
     streams = ((T.rl0[:], T.gath0[r], S.harr0, S.arr0, eng[0:K2]),
                (T.rla[:], T.gatha[r], S.harra, S.arra, eng[0:K2]),
                (T.rlb[:], T.gathb[r], S.harrb, S.arrb, eng[K2:2 * K2]))
@@ -80,7 +105,7 @@ def _relay_program(g, core, T, topo, r):
                                                srcs=[src], dsts=[dst for _ in mine], alu_op=0))
         g.wait_ge(landed, K1)
         g.remote_dma_fused(transfers, local_sem=S.hsent)
-    g.wait_ge(S.hsent, len(streams) * K2)
+    g.wait_ge(S.hsent, len(streams) * K2 + len(eng))
 
 
 def rank_program(g, core, T, topo):
@@ -93,30 +118,16 @@ def rank_program(g, core, T, topo):
     S = T.sem
     V, A, P, Q = g.vector, g.scalar, g.tensor, g.sync
     Act = ActivationFunctionType
-    tk = T.x.shape[1]
-    nt = N * tk
+    tk = TK
     half = tk // 2
     c_c, c_ic, c_ic2, c_q, c_s, c_r = [T.sc[:, i:i + 1] for i in range(6)]
-    w1, w2 = 1.0 / nt, (tk - 1.0) / nt
-    a1, a2 = math.sqrt(w1), math.sqrt(w2)
 
     Q.dma_start(T.xh[:], T.x[:, 0:2]).then_inc(S.ldh, 16)
     Q.dma_start(T.xs[:], T.x[:]).then_inc(S.ld, 16)
 
     V.memset(T.tabb[0:KB, :], 1.0).then_inc(S.cst, 1)
-    V.memset(T.wb[0:KB, 0:1], 0.0).then_inc(S.cst, 1)
     V.memset(T.taba[0:KA, :], 0.0).then_inc(S.cst, 1)
-    V.memset(T.wa[0:KA, 0:2 * N + 1], 0.0).then_inc(S.cst, 1)
-    V.wait_ge(S.cst, 4)
-    V.memset(T.wb[0:N, 0:1], 1.0 / nt).then_inc(S.cst, 1)
-    V.memset(T.wb[ROW2:KB, 0:1], EPS).then_inc(S.cst, 1)
-    V.memset(T.wa[0:N, 0:N], -a1 * w1).then_inc(S.cst, 1)
-    V.memset(T.wa[0:N, N:2 * N], -a2 * w1).then_inc(S.cst, 1)
-    V.memset(T.wa[0:N, 2 * N:2 * N + 1], -w1).then_inc(S.cst, 1)
-    V.memset(T.wa[ROW2:KA, 0:N], a1 * w2).then_inc(S.cst, 1)
-    V.memset(T.wa[ROW2:KA, N:2 * N], a2 * w2).then_inc(S.cst, 1)
-    V.memset(T.wa[ROW2:KA, 2 * N:2 * N + 1], w2).then_inc(S.cst, 1)
-    NCST = 12
+    NCST = 2
 
     A.wait_ge(S.ld, 16)
     A.activation(T.junk[:, 1:tk], T.xs[:, 1:tk], Act.Identity, scale=-1.0 / (tk - 1), accum_out=T.st[:, 0:1]).then_inc(S.a, 1)
@@ -132,10 +143,6 @@ def rank_program(g, core, T, topo):
     g.remote_dma(T.rla[:], T.st[:, 0:1], S.harra, S.sent, pid, rid, m1)
     g.wait_ge(S.a, 2)
     g.remote_dma(T.rlb[:], T.st[:, 4:5], S.harrb, S.sent, pid, rid, m1)
-    g.wait_ge(S.cst, NCST)
-    g.affine_select(T.wa[0:N, 0:N], T.wa[0:N, 0:N], [[-1, N]], AluOpType.not_equal, a1 * (1.0 - w1), 0, 1).then_inc(S.diag, 1)
-    g.affine_select(T.wa[ROW2:KA, N:2 * N], T.wa[ROW2:KA, N:2 * N], [[-1, N]], AluOpType.not_equal, -a2 * (1.0 - w2), 0,
-                    1).then_inc(S.diag, 1)
 
     A.wait_ge(S.a, 2)
     A.activation(c_c, T.st[:, 4:5], Act.Sqrt, bias=EPS, scale=1.0 / tk).then_inc(S.e, 1)
@@ -144,23 +151,22 @@ def rank_program(g, core, T, topo):
     V.wait_ge(S.e, 2)
     V.tensor_scalar(c_ic2, c_ic, c_ic, None, AluOpType.mult).then_inc(S.e, 1)
 
-    A.wait_ge(S.cst, NCST)
-    A.wait_ge(S.arr0, N)
-    A.dma_start(T.taba[0:N, :], T.gath0[:]).then_inc(S.gl0, 16)
     Q.wait_ge(S.cst, NCST)
+    Q.wait_ge(S.arr0, N)
+    Q.dma_start(T.taba[0:N, :], T.gath0[:]).then_inc(S.gl0, 16)
     Q.wait_ge(S.arra, N)
     Q.dma_start(T.taba[ROW2:KA, :], T.gatha[:]).then_inc(S.gla, 16)
     Q.wait_ge(S.arrb, N)
     Q.dma_start(T.tabb[0:N, :], T.gathb[:]).then_inc(S.glb, 16)
 
     P.wait_ge(S.cst, NCST)
-    P.wait_ge(S.diag, 2)
+    P.wait_ge(S.carr, 2 * K2)
     P.wait_ge(S.gl0, 16)
     P.wait_ge(S.gla, 16)
-    P.matmul(T.ps0[:, 0:2 * N], T.taba[0:KA, :], T.wa[0:KA, 0:2 * N], True, True).then_inc(S.mmd, 1)
-    P.matmul(T.ps1[:, 0:1], T.taba[0:KA, :], T.wa[0:KA, 2 * N:2 * N + 1], True, True).then_inc(S.mmn, 1)
+    P.matmul(T.ps0[:, 0:2 * N], T.taba[0:KA, :], T.wc[0:KA, 0:2 * N], True, True).then_inc(S.mmd, 1)
+    P.matmul(T.ps1[:, 0:1], T.taba[0:KA, :], T.wc[0:KA, 2 * N:2 * N + 1], True, True).then_inc(S.mmn, 1)
     P.wait_ge(S.glb, 16)
-    P.matmul(T.ps2[:, 0:1], T.tabb[0:KB, :], T.wb[0:KB, 0:1], True, True).then_inc(S.mmv, 1)
+    P.matmul(T.ps2[:, 0:1], T.tabb[0:KB, :], T.wc[0:KB, CB:CB + 1], True, True).then_inc(S.mmv, 1)
 
     A.wait_ge(S.e, 3)
     A.wait_ge(S.mmd, 1)

import math
from concourse.bass import DstId, RemoteDMATransfer
from concourse.mybir import AluOpType, ActivationFunctionType

N = 10
TK = 256
NT = N * TK
EPS = 0.01
W1, W2 = 1.0 / NT, (TK - 1.0) / NT
A1, A2 = math.sqrt(W1), math.sqrt(W2)
K1 = 8
K2 = 2
ROW2 = 32
KA = ROW2 + N
KB = ROW2 + 1
CB = 24

SCRATCH = {
    "xh": ("sbuf", [128, 2], "float32"),
    "xs": ("sbuf", [128, 256], "float32"),
    "xm": ("sbuf", [128, 256], "float32"),
    "ys": ("sbuf", [128, 256], "float32"),
    "junk": ("sbuf", [128, 256], "float32"),
    "j20": ("sbuf", [128, 24], "float32"),
    "st": ("sbuf", [128, 8], "float32"),
    "sc": ("sbuf", [128, 8], "float32"),
    "taba": ("sbuf", [128, 128], "float32"),
    "tabb": ("sbuf", [128, 128], "float32"),
    "wc": ("sbuf", [128, 28], "float32"),
    "rl0": ("dram", [128, 1], "float32"),
    "rla": ("dram", [128, 1], "float32"),
    "rlb": ("dram", [128, 1], "float32"),
    "gath0": ("dram", [N, 128, 1], "float32"),
    "gatha": ("dram", [N, 128, 1], "float32"),
    "gathb": ("dram", [N, 128, 1], "float32"),
    "ps0": ("psum", [128, 512], "float32"),
    "ps1": ("psum", [128, 512], "float32"),
    "ps2": ("psum", [128, 512], "float32"),
}
SEMAPHORES = ["ldh", "ld", "cst", "cs2", "diag", "carr", "a", "harr0", "harra", "harrb", "sent", "hsent", "arr0", "arra",
              "arrb", "gl0", "gla", "glb", "mmd", "mmn", "mmv", "e", "p", "si", "xmd", "y1", "y2", "stq"]


def _bits(mask):
    return [b for b in range(mask.bit_length()) if (mask >> b) & 1]


def _mask_of(bits):
    m = 0
    for b in bits:
        m |= 1 << b
    return m


def _relay_of(rank_core, cores, topo):
    hosts = max(topo.host(c) for c in cores) + 1
    cand = [c for c in range(hosts * topo.CORES_PER_HOST)
            if c not in cores and topo.host(c) == topo.host(rank_core) and topo.chip(c) == topo.chip(rank_core)
            and all(topo.may_write(c, d) for d in cores)]
    near = [c for c in cand if topo.die(c) == topo.die(rank_core)]
    return (near or cand)[0]


def _relay_program(g, core, T, topo, r):
    S = T.sem
    V = g.vector
    dests = list(T.cores)
    common = topo.mask(core, dests[0])
    for d in dests:
        common &= topo.mask(core, d)
    eng = _bits(common)
    eng = eng[::len(eng) // (2 * K2)][:2 * K2]

    V.memset(T.wc[:], 0.0).then_inc(S.cst, 1)
    V.wait_ge(S.cst, 1)
    V.memset(T.wc[0:N, 0:N], -A1 * W1).then_inc(S.cst, 1)
    V.memset(T.wc[ROW2:KA, N:2 * N], A2 * W2).then_inc(S.cst, 1)
    V.memset(T.wc[0:N, N:2 * N], -A2 * W1).then_inc(S.cs2, 1)
    V.memset(T.wc[ROW2:KA, 0:N], A1 * W2).then_inc(S.cs2, 1)
    V.memset(T.wc[0:N, 2 * N:2 * N + 1], -W1).then_inc(S.cs2, 1)
    V.memset(T.wc[ROW2:KA, 2 * N:2 * N + 1], W2).then_inc(S.cs2, 1)
    V.memset(T.wc[0:N, CB:CB + 1], 1.0 / NT).then_inc(S.cs2, 1)
    V.memset(T.wc[ROW2:KB, CB:CB + 1], EPS).then_inc(S.cs2, 1)
    g.wait_ge(S.cst, 3)
    g.affine_select(T.wc[0:N, 0:N], T.wc[0:N, 0:N], [[-1, N]], AluOpType.not_equal, A1 * (1.0 - W1), 0, 1).then_inc(S.diag, 1)
    g.affine_select(T.wc[ROW2:KA, N:2 * N], T.wc[ROW2:KA, N:2 * N], [[-1, N]], AluOpType.not_equal, -A2 * (1.0 - W2), 0,
                    1).then_inc(S.diag, 1)
    g.wait_ge(S.cs2, 6)
    g.wait_ge(S.diag, 2)
    rid, pid = topo.addr(T.cores[r], core)
    g.remote_dma(T.wc[:], T.wc[:], S.carr, S.hsent, pid, rid, _mask_of(eng))

    streams = ((T.rl0[:], T.gath0[r], S.harr0, S.arr0, eng[0:K2]),
               (T.rla[:], T.gatha[r], S.harra, S.arra, eng[0:K2]),
               (T.rlb[:], T.gathb[r], S.harrb, S.arrb, eng[K2:2 * K2]))
    for src, dst, landed, there, engines in streams:
        transfers = []
        for i, e in enumerate(engines):
            mine = dests[i::K2]
            ids = []
            for d in mine:
                rid, pid = topo.addr(d, core)
                ids.append(DstId(rid=rid, pnc=pid))
            transfers.append(RemoteDMATransfer(dst_ids=ids, dma_engine_mask=1 << e, remote_sem=there,
                                               srcs=[src], dsts=[dst for _ in mine], alu_op=0))
        g.wait_ge(landed, K1)
        g.remote_dma_fused(transfers, local_sem=S.hsent)
    g.wait_ge(S.hsent, len(streams) * K2 + len(eng))


def rank_program(g, core, T, topo):
    rank = T.rank_of(core)
    if rank is None:
        for r, c in enumerate(T.cores):
            if _relay_of(c, T.cores, topo) == core:
                _relay_program(g, core, T, topo, r)
        return
    S = T.sem
    V, A, P, Q = g.vector, g.scalar, g.tensor, g.sync
    Act = ActivationFunctionType
    tk = TK
    half = tk // 2
    c_c, c_ic, c_ic2, c_q, c_s, c_r = [T.sc[:, i:i + 1] for i in range(6)]

    Q.dma_start(T.xh[:], T.x[:, 0:2]).then_inc(S.ldh, 16)
    Q.dma_start(T.xs[:], T.x[:]).then_inc(S.ld, 16)

    V.memset(T.tabb[0:KB, :], 1.0).then_inc(S.cst, 1)
    V.memset(T.taba[0:KA, :], 0.0).then_inc(S.cst, 1)
    NCST = 2

    A.wait_ge(S.ld, 16)
    A.activation(T.junk[:, 1:tk], T.xs[:, 1:tk], Act.Identity, scale=-1.0 / (tk - 1), accum_out=T.st[:, 0:1]).then_inc(S.a, 1)
    A.wait_ge(S.a, 1)
    A.activation(T.junk[:, 1:tk], T.xs[:, 1:tk], Act.Square, bias=T.st[:, 0:1], accum_out=T.st[:, 4:5]).then_inc(S.a, 1)

    relay = _relay_of(core, T.cores, topo)
    rid, pid = topo.addr(relay, core)
    m1 = _mask_of(_bits(topo.mask(core, relay))[0:K1])
    g.wait_ge(S.ldh, 16)
    g.remote_dma(T.rl0[:], T.xh[:, 0:1], S.harr0, S.sent, pid, rid, m1)
    g.wait_ge(S.a, 1)
    g.remote_dma(T.rla[:], T.st[:, 0:1], S.harra, S.sent, pid, rid, m1)
    g.wait_ge(S.a, 2)
    g.remote_dma(T.rlb[:], T.st[:, 4:5], S.harrb, S.sent, pid, rid, m1)

    A.wait_ge(S.a, 2)
    A.activation(c_c, T.st[:, 4:5], Act.Sqrt, bias=EPS, scale=1.0 / tk).then_inc(S.e, 1)
    V.wait_ge(S.e, 1)
    V.reciprocal(c_ic, c_c).then_inc(S.e, 1)
    V.wait_ge(S.e, 2)
    V.tensor_scalar(c_ic2, c_ic, c_ic, None, AluOpType.mult).then_inc(S.e, 1)

    Q.wait_ge(S.cst, NCST)
    Q.wait_ge(S.arr0, N)
    Q.dma_start(T.taba[0:N, :], T.gath0[:]).then_inc(S.gl0, 16)
    Q.wait_ge(S.arra, N)
    Q.dma_start(T.taba[ROW2:KA, :], T.gatha[:]).then_inc(S.gla, 16)
    Q.wait_ge(S.arrb, N)
    Q.dma_start(T.tabb[0:N, :], T.gathb[:]).then_inc(S.glb, 16)

    P.wait_ge(S.cst, NCST)
    P.wait_ge(S.carr, 2 * K2)
    P.wait_ge(S.gl0, 16)
    P.wait_ge(S.gla, 16)
    P.matmul(T.ps0[:, 0:2 * N], T.taba[0:KA, :], T.wc[0:KA, 0:2 * N], True, True).then_inc(S.mmd, 1)
    P.matmul(T.ps1[:, 0:1], T.taba[0:KA, :], T.wc[0:KA, 2 * N:2 * N + 1], True, True).then_inc(S.mmn, 1)
    P.wait_ge(S.glb, 16)
    P.matmul(T.ps2[:, 0:1], T.tabb[0:KB, :], T.wc[0:KB, CB:CB + 1], True, True).then_inc(S.mmv, 1)

    A.wait_ge(S.e, 3)
    A.wait_ge(S.mmd, 1)
    A.activation(T.j20[:, 0:2 * N], T.ps0[:, 0:2 * N], Act.Square, scale=c_ic, accum_out=c_q).then_inc(S.p, 1)
    V.wait_ge(S.e, 3)
    V.wait_ge(S.mmn, 1)
    V.wait_ge(S.ld, 16)
    V.tensor_scalar(T.xm[:], T.xs[:], T.ps1[:, 0:1], c_ic, AluOpType.add, AluOpType.mult).then_inc(S.xmd, 1)

    A.wait_ge(S.p, 1)
    A.wait_ge(S.mmv, 1)
    A.activation(c_s, T.ps2[:, 0:1], Act.Sqrt, bias=c_q, scale=c_ic2).then_inc(S.p, 1)
    V.wait_ge(S.xmd, 1)
    V.wait_ge(S.p, 2)
    V.reciprocal(c_r, c_s).then_inc(S.si, 1)

    V.wait_ge(S.si, 1)
    V.tensor_scalar(T.ys[:, 0:half], T.xm[:, 0:half], c_r, None, AluOpType.mult).then_inc(S.y1, 1)
    A.wait_ge(S.si, 1)
    A.wait_ge(S.xmd, 1)
    A.activation(T.ys[:, half:tk], T.xm[:, half:tk], Act.Identity, scale=c_r).then_inc(S.y2, 1)

    Q.wait_ge(S.y1, 1)
    Q.wait_ge(S.y2, 1)
    Q.dma_start(T.y[:], T.ys[:]).then_inc(S.stq, 16)
    Q.wait_ge(S.stq, 16)
    g.wait_ge(S.sent, 3 * K1)
